import numpy as np
import ml_dtypes


def mxq(x, axis, fmt="e4m3"):
    dtype, down = {"e4m3": (ml_dtypes.float8_e4m3fn, 7), "e5m2": (ml_dtypes.float8_e5m2, 14)}[fmt]
    v = np.moveaxis(np.asarray(x, np.float32).astype(ml_dtypes.bfloat16).astype(np.float64), axis, -1)
    blocks = v.reshape(v.shape[:-1] + (-1, 32))
    amax = np.abs(blocks).max(-1, keepdims=True)
    byte = np.maximum(np.where(amax > 0, np.frexp(amax)[1] - 1 + 127, 0) - down, 1)
    scale = np.exp2(byte - 127.0)
    codes = (blocks / scale).astype(np.float32).astype(dtype).astype(np.float64)
    return np.moveaxis((codes * scale).reshape(v.shape), -1, axis)


WIDE = False


def mx_kscale(k):
    if not WIDE:
        return np.ones(k)
    levels = np.array([10, -10, 5, -5, 0])
    if k % 512:
        return np.exp2(np.random.permutation(np.resize(levels, k // 32))).repeat(32)
    a = np.empty((k // 512, 16))
    for p in range(k // 512):
        a[p, :8] = np.random.permutation(np.resize(levels, 8))
        for g in range(8):
            far = levels[np.abs(levels - a[p, g]) >= 10]
            a[p, g + 8] = far[np.random.randint(len(far))]
    return np.exp2(a.ravel()).repeat(32)


def f64(x):
    return np.asarray(x).astype(np.float64)


def striped(idx):
    return np.tile(idx.reshape(-1, 16).T, (8, 1)).astype(np.uint16)


def unstriped(offs):
    return offs[:16].T.reshape(-1).astype(np.int64)


def relu2(v):
    return np.maximum(v, 0.0) ** 2


K, T, S, N = 512, 4096, 1536, 128


def setup_inputs():
    n = np.random.standard_normal
    s = mx_kscale(K)[:, None]
    return {
        "xT": (n((K, T)) * s).astype(np.float32),
        "w": (n((K, N)) / np.sqrt(K) / s).astype(np.float32),
        "b": (0.3 * n((N, 1))).astype(np.float32),
        "offs": striped(np.random.permutation(T)[:S]),
    }


def reference(xT, w, b, offs):
    idx = unstriped(offs)
    xq = mxq(f64(xT)[:, idx], 0, "e4m3")
    y = mxq(f64(w), 0, "e4m3").T @ xq
    y = relu2(y + f64(b))
    return y

@@ -1,0 +1,137 @@
+from contextlib import ExitStack
+
+import concourse.mybir as mybir
+
+K, T, S, N = 512, 4096, 1536, 128
+P = 128
+PACK = 4
+SLICE = 512
+HALF = 256
+
+FLOPS = 2 * K * N * S
+
+F32 = mybir.dt.float32
+BF16 = mybir.dt.bfloat16
+U32 = mybir.dt.uint32
+U16 = mybir.dt.uint16
+U8 = mybir.dt.uint8
+FP8X4 = mybir.dt.float8_e4m3fn_x4
+RELU = mybir.ActivationFunctionType.Relu
+SQUARE = mybir.ActivationFunctionType.Square
+ADD = mybir.AluOpType.add
+MAX = mybir.AluOpType.max
+MULT = mybir.AluOpType.mult
+
+
+def tile_picked_pick_lin_relu2_sub_e_kernel(tc, xT, w, b, offs, out):
+    nc = tc.nc
+    with ExitStack() as ctx:
+        keep = ctx.enter_context(tc.tile_pool(name="keep", bufs=1))
+        psum = ctx.enter_context(tc.psum_pool(name="psum", bufs=1))
+
+        offsets = keep.tile([P, S // 16], U16, name="offsets")
+        planes = [keep.tile([P, T], F32, name=f"plane{t}") for t in range(PACK)]
+        w_raw = keep.tile([P, PACK, N], F32, name="w_raw")
+        bias = keep.tile([P, 1], F32, name="bias")
+        warm = keep.tile([P, 1], F32, name="warm")
+
+        x_rows = xT.rearrange("(p j) n -> p j n", j=PACK)
+        nc.sync.dma_start(planes[0][:], x_rows[:, 0, :])
+        nc.sync.dma_start(offsets[:], offs)
+        for t in range(1, PACK):
+            nc.sync.dma_start(planes[t][:], x_rows[:, t, :])
+        nc.sync.dma_start(w_raw[:], w.rearrange("(p j) m -> p j m", j=PACK))
+        nc.scalar.dma_start(bias[:], b)
+
+        nc.vector.memset(warm[:], 0.0)
+        nc.scalar.activation(warm[:], warm[:], RELU)
+
+        g01 = [keep.tile([P, 2, SLICE], F32, name=f"g01_{s}") for s in range(2)]
+        g2 = keep.tile([P, SLICE], F32, name="g2")
+        g3 = keep.tile([P, SLICE], F32, name="g3")
+        grouped = [keep.tile([P, SLICE, PACK], BF16, name=f"grouped{s}", align_bytes=64) for s in range(3)]
+        codes = [keep.tile([P, SLICE], U32, name=f"codes{s}", align_bytes=64) for s in range(3)]
+        scales = [keep.tile([P, SLICE], U8, name=f"scales{s}", align_bytes=64) for s in range(3)]
+        w_grouped = keep.tile([P, N, PACK], BF16, name="w_grouped", align_bytes=64)
+        w_codes = keep.tile([P, N], U32, name="w_codes", align_bytes=64)
+        w_scales = keep.tile([P, N], U8, name="w_scales", align_bytes=64)
+        kept = keep.tile([P, S], F32, name="kept")
+        result = keep.tile([P, S], F32, name="result")
+        accs = [psum.tile([P, SLICE], F32, name=f"acc{i}") for i in range(6)]
+
+        def list_part(s):
+            return offsets[:, s * SLICE // 16 : (s + 1) * SLICE // 16]
+
+        def quantise(s, a, z):
+            nc.vector.quantize_mx(
+                out=codes[s][:, a:z].bitcast(FP8X4),
+                scales=scales[s][:, a:z],
+                in_=grouped[s][:].rearrange("p n j -> p (n j)")[:, PACK * a : PACK * z],
+            )
+
+        def product(i, s, a, z):
+            nc.tensor.matmul_mx(
+                out=accs[i][:, 0 : z - a],
+                lhsT=w_codes[:].bitcast(FP8X4),
+                lhsT_scale=w_scales[:],
+                rhs=codes[s][:, a:z].bitcast(FP8X4),
+                rhs_scale=scales[s][:, a:z],
+                start=True,
+                stop=True,
+            )
+
+        def relu_s(i, c, n):
+            nc.scalar.activation(kept[:, c : c + n], accs[i][:, 0:n], RELU, bias=bias[:])
+
+        def square_s(c, n):
+            nc.scalar.activation(result[:, c : c + n], kept[:, c : c + n], SQUARE)
+
+        def relu_v(i, c, n):
+            nc.vector.tensor_scalar(kept[:, c : c + n], accs[i][:, 0:n], bias[:], 0.0, ADD, MAX)
+
+        def square_v(c, n):
+            nc.vector.tensor_tensor(result[:, c : c + n], kept[:, c : c + n], kept[:, c : c + n], MULT)
+
+        def store(queue, c, n):
+            queue.dma_start(out[:, c : c + n], result[:, c : c + n])
+
+        def gather(target, t, s):
+            nc.vector.tensor_copy(target, planes[t][:].indirect(list_part(s)))
+
+        for t in range(2):
+            for s in range(2):
+                gather(g01[s][:, t, :], t, s)
+            gather(grouped[2][:, :, t], t, 2)
+        for s in range(2):
+            nc.scalar.copy(grouped[s][:, :, 0:2], g01[s][:].rearrange("p t n -> p n t"))
+        gather(g2[:], 2, 0)
+        nc.scalar.copy(grouped[0][:, :, 2], g2[:])
+        for s in (1, 2):
+            gather(grouped[s][:, :, 2], 2, s)
+
+        nc.gpsimd.tensor_copy(w_grouped[:], w_raw[:].rearrange("p j m -> p m j"))
+        gather(grouped[2][:, :, 3], 3, 2)
+        gather(g3[:], 3, 0)
+        nc.scalar.copy(grouped[0][:, :, 3], g3[:])
+        nc.vector.quantize_mx(
+            out=w_codes[:].bitcast(FP8X4), scales=w_scales[:], in_=w_grouped[:].rearrange("p m j -> p (m j)")
+        )
+        quantise(2, 0, SLICE)
+        product(4, 2, 0, SLICE)
+        gather(grouped[1][:, :, 3], 3, 1)
+        relu_s(4, 2 * SLICE, SLICE)
+        square_s(2 * SLICE, SLICE)
+        store(nc.sync, 2 * SLICE, SLICE)
+        for s in range(2):
+            quantise(s, 0, SLICE)
+            for h in range(2):
+                product(2 * s + h, s, h * HALF, (h + 1) * HALF)
+        for s in range(2):
+            relu_s(2 * s, s * SLICE, HALF)
+            square_s(s * SLICE, HALF)
+            store(nc.sync, s * SLICE, HALF)
+        for s in range(2):
+            relu_v(2 * s + 1, s * SLICE + HALF, HALF)
+        for s in range(2):
+            square_v(s * SLICE + HALF, HALF)
+            store(nc.sync, s * SLICE + HALF, HALF)

@@ -16,11 +16,14 @@ U32 = mybir.dt.uint32
 U16 = mybir.dt.uint16
 U8 = mybir.dt.uint8
 FP8X4 = mybir.dt.float8_e4m3fn_x4
+COPY = mybir.ActivationFunctionType.Copy
 RELU = mybir.ActivationFunctionType.Relu
 SQUARE = mybir.ActivationFunctionType.Square
 ADD = mybir.AluOpType.add
 MAX = mybir.AluOpType.max
 MULT = mybir.AluOpType.mult
+
+CHUNKS = ((2048, 2048), (2048, 2048), (2048, 1280, 768), (2048, 1024, 512, 512))
 
 
 def tile_picked_pick_lin_relu2_sub_e_kernel(tc, xT, w, b, offs, out):
@@ -31,24 +34,26 @@ def tile_picked_pick_lin_relu2_sub_e_kernel(tc, xT, w, b, offs, out):
 
         offsets = keep.tile([P, S // 16], U16, name="offsets")
         planes = [keep.tile([P, T], F32, name=f"plane{t}") for t in range(PACK)]
+        rounded = [keep.tile([P, T], BF16, name=f"rounded{t}") for t in range(PACK)]
         w_raw = keep.tile([P, PACK, N], F32, name="w_raw")
         bias = keep.tile([P, 1], F32, name="bias")
         warm = keep.tile([P, 1], F32, name="warm")
 
+        def chunks(t):
+            return [slice(sum(CHUNKS[t][:i]), sum(CHUNKS[t][: i + 1])) for i in range(len(CHUNKS[t]))]
+
         x_rows = xT.rearrange("(p j) n -> p j n", j=PACK)
-        nc.sync.dma_start(planes[0][:], x_rows[:, 0, :])
-        nc.sync.dma_start(offsets[:], offs)
-        for t in range(1, PACK):
-            nc.sync.dma_start(planes[t][:], x_rows[:, t, :])
+        for t in range(PACK):
+            for i, cols in enumerate(chunks(t)):
+                nc.sync.dma_start(planes[t][:, cols], x_rows[:, t, cols])
+                if (t, i) == (0, 0):
+                    nc.sync.dma_start(offsets[:], offs)
         nc.sync.dma_start(w_raw[:], w.rearrange("(p j) m -> p j m", j=PACK))
         nc.scalar.dma_start(bias[:], b)
 
         nc.vector.memset(warm[:], 0.0)
         nc.scalar.activation(warm[:], warm[:], RELU)
 
-        g01 = [keep.tile([P, 2, SLICE], F32, name=f"g01_{s}") for s in range(2)]
-        g2 = keep.tile([P, SLICE], F32, name="g2")
-        g3 = keep.tile([P, SLICE], F32, name="g3")
         grouped = [keep.tile([P, SLICE, PACK], BF16, name=f"grouped{s}", align_bytes=64) for s in range(3)]
         codes = [keep.tile([P, SLICE], U32, name=f"codes{s}", align_bytes=64) for s in range(3)]
         scales = [keep.tile([P, SLICE], U8, name=f"scales{s}", align_bytes=64) for s in range(3)]
@@ -95,43 +100,29 @@ def tile_picked_pick_lin_relu2_sub_e_kernel(tc, xT, w, b, offs, out):
         def store(queue, c, n):
             queue.dma_start(out[:, c : c + n], result[:, c : c + n])
 
-        def gather(target, t, s):
-            nc.vector.tensor_copy(target, planes[t][:].indirect(list_part(s)))
+        for t in range(PACK):
+            for cols in chunks(t):
+                nc.vector.tensor_copy(rounded[t][:, cols], planes[t][:, cols])
+            nc.vector.tensor_copy(grouped[0][:, :, t], planes[t][:].indirect(list_part(0)))
+            for s in (1, 2):
+                nc.scalar.activation(grouped[s][:, :, t], rounded[t][:].indirect(list_part(s)), COPY)
 
-        for t in range(2):
-            for s in range(2):
-                gather(g01[s][:, t, :], t, s)
-            gather(grouped[2][:, :, t], t, 2)
-        for s in range(2):
-            nc.scalar.copy(grouped[s][:, :, 0:2], g01[s][:].rearrange("p t n -> p n t"))
-        gather(g2[:], 2, 0)
-        nc.scalar.copy(grouped[0][:, :, 2], g2[:])
-        for s in (1, 2):
-            gather(grouped[s][:, :, 2], 2, s)
-
-        nc.gpsimd.tensor_copy(w_grouped[:], w_raw[:].rearrange("p j m -> p m j"))
-        gather(grouped[2][:, :, 3], 3, 2)
-        gather(g3[:], 3, 0)
-        nc.scalar.copy(grouped[0][:, :, 3], g3[:])
+        nc.gpsimd.tensor_scalar(w_grouped[:], w_raw[:].rearrange("p j m -> p m j"), 1.0, 0.0, MULT, ADD)
         nc.vector.quantize_mx(
             out=w_codes[:].bitcast(FP8X4), scales=w_scales[:], in_=w_grouped[:].rearrange("p m j -> p (m j)")
         )
-        quantise(2, 0, SLICE)
-        product(4, 2, 0, SLICE)
-        gather(grouped[1][:, :, 3], 3, 1)
-        relu_s(4, 2 * SLICE, SLICE)
-        square_s(2 * SLICE, SLICE)
-        store(nc.sync, 2 * SLICE, SLICE)
         for s in range(2):
             quantise(s, 0, SLICE)
             for h in range(2):
                 product(2 * s + h, s, h * HALF, (h + 1) * HALF)
-        for s in range(2):
-            relu_s(2 * s, s * SLICE, HALF)
-            square_s(s * SLICE, HALF)
-            store(nc.sync, s * SLICE, HALF)
-        for s in range(2):
-            relu_v(2 * s + 1, s * SLICE + HALF, HALF)
-        for s in range(2):
-            square_v(s * SLICE + HALF, HALF)
-            store(nc.sync, s * SLICE + HALF, HALF)
+        for h in range(2):
+            quantise(2, h * HALF, (h + 1) * HALF)
+            product(4 + h, 2, h * HALF, (h + 1) * HALF)
+        for i in range(6):
+            if i % 2 == 0:
+                relu_v(i, i * HALF, HALF)
+                square_v(i * HALF, HALF)
+            else:
+                relu_s(i, i * HALF, HALF)
+                square_s(i * HALF, HALF)
+            store(nc.sync, i * HALF, HALF)

@@ -23,7 +23,9 @@ ADD = mybir.AluOpType.add
 MAX = mybir.AluOpType.max
 MULT = mybir.AluOpType.mult
 
-CHUNKS = ((2048, 2048), (2048, 2048), (2048, 1280, 768), (2048, 1024, 512, 512))
+CHUNKS = ((2560, 1536), (2560, 1536), (2560, 1536), (2304, 1024, 768))
+V_SHARE = 640
+S_SHARE = S - V_SHARE
 
 
 def tile_picked_pick_lin_relu2_sub_e_kernel(tc, xT, w, b, offs, out):
@@ -40,89 +42,103 @@ def tile_picked_pick_lin_relu2_sub_e_kernel(tc, xT, w, b, offs, out):
         warm = keep.tile([P, 1], F32, name="warm")
 
         def chunks(t):
-            return [slice(sum(CHUNKS[t][:i]), sum(CHUNKS[t][: i + 1])) for i in range(len(CHUNKS[t]))]
+            return [(sum(CHUNKS[t][:i]), sum(CHUNKS[t][: i + 1])) for i in range(len(CHUNKS[t]))]
 
         x_rows = xT.rearrange("(p j) n -> p j n", j=PACK)
         for t in range(PACK):
-            for i, cols in enumerate(chunks(t)):
-                nc.sync.dma_start(planes[t][:, cols], x_rows[:, t, cols])
-                if (t, i) == (0, 0):
+            for a, z in chunks(t):
+                nc.sync.dma_start(planes[t][:, a:z], x_rows[:, t, a:z])
+                if (t, a) == (0, 0):
                     nc.sync.dma_start(offsets[:], offs)
         nc.sync.dma_start(w_raw[:], w.rearrange("(p j) m -> p j m", j=PACK))
-        nc.scalar.dma_start(bias[:], b)
+        nc.sync.dma_start(bias[:], b)
 
         nc.vector.memset(warm[:], 0.0)
         nc.scalar.activation(warm[:], warm[:], RELU)
 
-        grouped = [keep.tile([P, SLICE, PACK], BF16, name=f"grouped{s}", align_bytes=64) for s in range(3)]
-        codes = [keep.tile([P, SLICE], U32, name=f"codes{s}", align_bytes=64) for s in range(3)]
-        scales = [keep.tile([P, SLICE], U8, name=f"scales{s}", align_bytes=64) for s in range(3)]
-        w_grouped = keep.tile([P, N, PACK], BF16, name="w_grouped", align_bytes=64)
+        grouped_v = keep.tile([P, V_SHARE, PACK], BF16, name="grouped_v", tag="after_v", align_bytes=64)
+        grouped_s = keep.tile([P, S_SHARE, PACK], BF16, name="grouped_s", align_bytes=64)
+        w_grouped = keep.tile([P, N, PACK], BF16, name="w_grouped", tag="after_w", align_bytes=64)
         w_codes = keep.tile([P, N], U32, name="w_codes", align_bytes=64)
         w_scales = keep.tile([P, N], U8, name="w_scales", align_bytes=64)
+        scales = keep.tile([P, S], U8, name="scales", align_bytes=64)
         kept = keep.tile([P, S], F32, name="kept")
         result = keep.tile([P, S], F32, name="result")
-        accs = [psum.tile([P, SLICE], F32, name=f"acc{i}") for i in range(6)]
-
-        def list_part(s):
-            return offsets[:, s * SLICE // 16 : (s + 1) * SLICE // 16]
-
-        def quantise(s, a, z):
-            nc.vector.quantize_mx(
-                out=codes[s][:, a:z].bitcast(FP8X4),
-                scales=scales[s][:, a:z],
-                in_=grouped[s][:].rearrange("p n j -> p (n j)")[:, PACK * a : PACK * z],
-            )
-
-        def product(i, s, a, z):
-            nc.tensor.matmul_mx(
-                out=accs[i][:, 0 : z - a],
-                lhsT=w_codes[:].bitcast(FP8X4),
-                lhsT_scale=w_scales[:],
-                rhs=codes[s][:, a:z].bitcast(FP8X4),
-                rhs_scale=scales[s][:, a:z],
-                start=True,
-                stop=True,
-            )
-
-        def relu_s(i, c, n):
-            nc.scalar.activation(kept[:, c : c + n], accs[i][:, 0:n], RELU, bias=bias[:])
-
-        def square_s(c, n):
-            nc.scalar.activation(result[:, c : c + n], kept[:, c : c + n], SQUARE)
-
-        def relu_v(i, c, n):
-            nc.vector.tensor_scalar(kept[:, c : c + n], accs[i][:, 0:n], bias[:], 0.0, ADD, MAX)
-
-        def square_v(c, n):
-            nc.vector.tensor_tensor(result[:, c : c + n], kept[:, c : c + n], kept[:, c : c + n], MULT)
-
-        def store(queue, c, n):
-            queue.dma_start(out[:, c : c + n], result[:, c : c + n])
 
         for t in range(PACK):
-            for cols in chunks(t):
-                nc.vector.tensor_copy(rounded[t][:, cols], planes[t][:, cols])
-            nc.vector.tensor_copy(grouped[0][:, :, t], planes[t][:].indirect(list_part(0)))
-            for s in (1, 2):
-                nc.scalar.activation(grouped[s][:, :, t], rounded[t][:].indirect(list_part(s)), COPY)
+            for a, z in chunks(t):
+                cut = z - (z - a) // 3 if z == T else z
+                nc.vector.tensor_copy(rounded[t][:, a:cut], planes[t][:, a:cut])
+                if cut < z:
+                    nc.scalar.activation(rounded[t][:, cut:z], planes[t][:, cut:z], COPY)
+            nc.vector.tensor_copy(grouped_v[:, :, t], planes[t][:].indirect(offsets[:, 0 : V_SHARE // 16]))
+            nc.scalar.activation(grouped_s[:, :, t], rounded[t][:].indirect(offsets[:, V_SHARE // 16 : S // 16]), COPY)
 
         nc.gpsimd.tensor_scalar(w_grouped[:], w_raw[:].rearrange("p j m -> p m j"), 1.0, 0.0, MULT, ADD)
         nc.vector.quantize_mx(
             out=w_codes[:].bitcast(FP8X4), scales=w_scales[:], in_=w_grouped[:].rearrange("p m j -> p (m j)")
         )
-        for s in range(2):
-            quantise(s, 0, SLICE)
-            for h in range(2):
-                product(2 * s + h, s, h * HALF, (h + 1) * HALF)
-        for h in range(2):
-            quantise(2, h * HALF, (h + 1) * HALF)
-            product(4 + h, 2, h * HALF, (h + 1) * HALF)
-        for i in range(6):
-            if i % 2 == 0:
-                relu_v(i, i * HALF, HALF)
-                square_v(i * HALF, HALF)
-            else:
-                relu_s(i, i * HALF, HALF)
-                square_s(i * HALF, HALF)
-            store(nc.sync, i * HALF, HALF)
+
+        def product(codes, grouped, first, c, n):
+            nc.vector.quantize_mx(
+                out=codes.bitcast(FP8X4),
+                scales=scales[:, c : c + n],
+                in_=grouped[:].rearrange("p n j -> p (n j)")[:, PACK * (c - first) : PACK * (c - first + n)],
+            )
+            acc = psum.tile([P, SLICE], F32, name=f"acc{c}")
+            nc.tensor.matmul_mx(
+                out=acc[:, 0:n],
+                lhsT=w_codes[:].bitcast(FP8X4),
+                lhsT_scale=w_scales[:],
+                rhs=codes.bitcast(FP8X4),
+                rhs_scale=scales[:, c : c + n],
+                start=True,
+                stop=True,
+            )
+            return acc[:, 0:n]
+
+        def relu_s(c, n):
+            nc.scalar.activation(kept[:, c : c + n], accs[c], RELU, bias=bias[:])
+
+        def square_s(c, n):
+            nc.scalar.activation(result[:, c : c + n], kept[:, c : c + n], SQUARE)
+
+        def relu_v(c, n):
+            nc.vector.tensor_scalar(kept[:, c : c + n], accs[c], bias[:], 0.0, ADD, MAX)
+
+        def square_v(c, n):
+            nc.vector.tensor_tensor(result[:, c : c + n], kept[:, c : c + n], kept[:, c : c + n], MULT)
+
+        def square_g(c, n):
+            nc.gpsimd.tensor_tensor(result[:, c : c + n], kept[:, c : c + n], kept[:, c : c + n], MULT)
+
+        def store(queue, c, n):
+            queue.dma_start(out[:, c : c + n], result[:, c : c + n])
+
+        accs = {}
+        codes_first = keep.tile([P, 256], U32, name="codes_first", align_bytes=64)
+        accs[0] = product(codes_first[:], grouped_v, 0, 0, 256)
+        codes_v = keep.tile([P, 384], U32, name="codes_v", tag="after_w", align_bytes=64)
+        accs[256] = product(codes_v[:, 0:256], grouped_v, 0, 256, 256)
+        accs[512] = product(codes_v[:, 256:384], grouped_v, 0, 512, 128)
+        codes_s = keep.tile([P, S_SHARE], U32, name="codes_s", tag="after_v", align_bytes=64)
+        for c, n in ((640, 256), (1024, 256), (1280, 256), (896, 128)):
+            accs[c] = product(codes_s[:, c - V_SHARE : c - V_SHARE + n], grouped_s, V_SHARE, c, n)
+
+        relu_s(0, 256)
+        relu_s(256, 256)
+        square_s(0, 256)
+        relu_s(512, 128)
+        square_s(256, 384)
+        store(nc.sync, 0, 640)
+        relu_s(640, 256)
+        relu_v(1024, 256)
+        relu_v(1280, 256)
+        relu_s(896, 128)
+        square_v(1024, 256)
+        store(nc.sync, 1024, 256)
+        square_s(640, 256)
+        square_s(896, 128)
+        store(nc.scalar, 640, 384)
+        square_v(1280, 256)
+        store(nc.sync, 1280, 256)

@@ -23,9 +23,7 @@ ADD = mybir.AluOpType.add
 MAX = mybir.AluOpType.max
 MULT = mybir.AluOpType.mult
 
-CHUNKS = ((2560, 1536), (2560, 1536), (2560, 1536), (2304, 1024, 768))
-V_SHARE = 640
-S_SHARE = S - V_SHARE
+CHUNKS = ((3072, 1024), (2560, 1536), (2560, 1536), (2304, 1024, 768))
 
 
 def tile_picked_pick_lin_relu2_sub_e_kernel(tc, xT, w, b, offs, out):
@@ -56,9 +54,9 @@ def tile_picked_pick_lin_relu2_sub_e_kernel(tc, xT, w, b, offs, out):
         nc.vector.memset(warm[:], 0.0)
         nc.scalar.activation(warm[:], warm[:], RELU)
 
-        grouped_v = keep.tile([P, V_SHARE, PACK], BF16, name="grouped_v", tag="after_v", align_bytes=64)
-        grouped_s = keep.tile([P, S_SHARE, PACK], BF16, name="grouped_s", align_bytes=64)
-        w_grouped = keep.tile([P, N, PACK], BF16, name="w_grouped", tag="after_w", align_bytes=64)
+        grouped = [keep.tile([P, SLICE, PACK], BF16, name=f"grouped{s}", align_bytes=64) for s in range(3)]
+        codes = {}
+        w_grouped = keep.tile([P, N, PACK], BF16, name="w_grouped", align_bytes=64)
         w_codes = keep.tile([P, N], U32, name="w_codes", align_bytes=64)
         w_scales = keep.tile([P, N], U8, name="w_scales", align_bytes=64)
         scales = keep.tile([P, S], U8, name="scales", align_bytes=64)
@@ -67,30 +65,35 @@ def tile_picked_pick_lin_relu2_sub_e_kernel(tc, xT, w, b, offs, out):
 
         for t in range(PACK):
             for a, z in chunks(t):
-                cut = z - (z - a) // 3 if z == T else z
+                cut = z - (z - a) // 48 * 16 if z == T else z
                 nc.vector.tensor_copy(rounded[t][:, a:cut], planes[t][:, a:cut])
                 if cut < z:
                     nc.scalar.activation(rounded[t][:, cut:z], planes[t][:, cut:z], COPY)
-            nc.vector.tensor_copy(grouped_v[:, :, t], planes[t][:].indirect(offsets[:, 0 : V_SHARE // 16]))
-            nc.scalar.activation(grouped_s[:, :, t], rounded[t][:].indirect(offsets[:, V_SHARE // 16 : S // 16]), COPY)
+            nc.vector.tensor_copy(grouped[0][:, :, t], planes[t][:].indirect(offsets[:, 0 : SLICE // 16]))
+            for s in (1, 2):
+                part = offsets[:, s * SLICE // 16 : (s + 1) * SLICE // 16]
+                nc.scalar.activation(grouped[s][:, :, t], rounded[t][:].indirect(part), COPY)
 
-        nc.gpsimd.tensor_scalar(w_grouped[:], w_raw[:].rearrange("p j m -> p m j"), 1.0, 0.0, MULT, ADD)
+        nc.vector.tensor_copy(w_grouped[:], w_raw[:].rearrange("p j m -> p m j"))
         nc.vector.quantize_mx(
             out=w_codes[:].bitcast(FP8X4), scales=w_scales[:], in_=w_grouped[:].rearrange("p m j -> p (m j)")
         )
 
-        def product(codes, grouped, first, c, n):
+        def product(c, n):
+            s, a = divmod(c, SLICE)
+            if a == 0:
+                codes[s] = keep.tile([P, SLICE], U32, name=f"codes{s}", tag="codes", bufs=2, align_bytes=64)
             nc.vector.quantize_mx(
-                out=codes.bitcast(FP8X4),
+                out=codes[s][:, a : a + n].bitcast(FP8X4),
                 scales=scales[:, c : c + n],
-                in_=grouped[:].rearrange("p n j -> p (n j)")[:, PACK * (c - first) : PACK * (c - first + n)],
+                in_=grouped[s][:].rearrange("p n j -> p (n j)")[:, PACK * a : PACK * (a + n)],
             )
             acc = psum.tile([P, SLICE], F32, name=f"acc{c}")
             nc.tensor.matmul_mx(
                 out=acc[:, 0:n],
                 lhsT=w_codes[:].bitcast(FP8X4),
                 lhsT_scale=w_scales[:],
-                rhs=codes.bitcast(FP8X4),
+                rhs=codes[s][:, a : a + n].bitcast(FP8X4),
                 rhs_scale=scales[:, c : c + n],
                 start=True,
                 stop=True,
@@ -109,36 +112,30 @@ def tile_picked_pick_lin_relu2_sub_e_kernel(tc, xT, w, b, offs, out):
         def square_v(c, n):
             nc.vector.tensor_tensor(result[:, c : c + n], kept[:, c : c + n], kept[:, c : c + n], MULT)
 
-        def square_g(c, n):
-            nc.gpsimd.tensor_tensor(result[:, c : c + n], kept[:, c : c + n], kept[:, c : c + n], MULT)
-
         def store(queue, c, n):
             queue.dma_start(out[:, c : c + n], result[:, c : c + n])
 
         accs = {}
-        codes_first = keep.tile([P, 256], U32, name="codes_first", align_bytes=64)
-        accs[0] = product(codes_first[:], grouped_v, 0, 0, 256)
-        codes_v = keep.tile([P, 384], U32, name="codes_v", tag="after_w", align_bytes=64)
-        accs[256] = product(codes_v[:, 0:256], grouped_v, 0, 256, 256)
-        accs[512] = product(codes_v[:, 256:384], grouped_v, 0, 512, 128)
-        codes_s = keep.tile([P, S_SHARE], U32, name="codes_s", tag="after_v", align_bytes=64)
-        for c, n in ((640, 256), (1024, 256), (1280, 256), (896, 128)):
-            accs[c] = product(codes_s[:, c - V_SHARE : c - V_SHARE + n], grouped_s, V_SHARE, c, n)
+        for c, n in ((0, 256), (256, 256), (512, 256), (768, 256)):
+            accs[c] = product(c, n)
+        relu_v(0, 256)
+        for c, n in ((1024, 256), (1280, 128), (1408, 128)):
+            accs[c] = product(c, n)
 
-        relu_s(0, 256)
         relu_s(256, 256)
-        square_s(0, 256)
-        relu_s(512, 128)
-        square_s(256, 384)
-        store(nc.sync, 0, 640)
-        relu_s(640, 256)
-        relu_v(1024, 256)
-        relu_v(1280, 256)
-        relu_s(896, 128)
-        square_v(1024, 256)
-        store(nc.sync, 1024, 256)
-        square_s(640, 256)
-        square_s(896, 128)
-        store(nc.scalar, 640, 384)
-        square_v(1280, 256)
-        store(nc.sync, 1280, 256)
+        relu_s(512, 256)
+        square_s(0, 512)
+        store(nc.sync, 0, 512)
+        relu_v(768, 256)
+        square_v(512, 256)
+        store(nc.sync, 512, 256)
+        relu_s(1024, 256)
+        relu_s(1280, 128)
+        relu_v(1408, 128)
+        square_v(768, 256)
+        store(nc.sync, 768, 256)
+        square_s(1024, 256)
+        square_s(1280, 128)
+        store(nc.scalar, 1024, 384)
+        square_v(1408, 128)
+        store(nc.sync, 1408, 128)

@@ -5,8 +5,8 @@ import concourse.mybir as mybir
 K, T, S, N = 512, 4096, 1536, 128
 P = 128
 PACK = 4
-SLICE = 512
-HALF = 256
+PART = 512
+LIST_ROWS = 16
 
 FLOPS = 2 * K * N * S
 
@@ -23,7 +23,11 @@ ADD = mybir.AluOpType.add
 MAX = mybir.AluOpType.max
 MULT = mybir.AluOpType.mult
 
-CHUNKS = ((3072, 1024), (2560, 1536), (2560, 1536), (2304, 1024, 768))
+CHUNKS = ((3072, 1024), (2816, 1280), (2816, 1280), (2304, 1280, 512))
+SCALAR_ROUNDS = (336, 0, 0, 0)
+
+EARLY_PIECES = ((0, 256), (256, 256), (512, 256), (768, 256))
+LATE_PIECES = ((1024, 256), (1280, 128), (1408, 128))
 
 
 def tile_picked_pick_lin_relu2_sub_e_kernel(tc, xT, w, b, offs, out):
@@ -32,12 +36,11 @@ def tile_picked_pick_lin_relu2_sub_e_kernel(tc, xT, w, b, offs, out):
         keep = ctx.enter_context(tc.tile_pool(name="keep", bufs=1))
         psum = ctx.enter_context(tc.psum_pool(name="psum", bufs=1))
 
-        offsets = keep.tile([P, S // 16], U16, name="offsets")
+        offsets = keep.tile([P, S // LIST_ROWS], U16, name="offsets")
         planes = [keep.tile([P, T], F32, name=f"plane{t}") for t in range(PACK)]
         rounded = [keep.tile([P, T], BF16, name=f"rounded{t}") for t in range(PACK)]
         w_raw = keep.tile([P, PACK, N], F32, name="w_raw")
         bias = keep.tile([P, 1], F32, name="bias")
-        warm = keep.tile([P, 1], F32, name="warm")
 
         def chunks(t):
             return [(sum(CHUNKS[t][:i]), sum(CHUNKS[t][: i + 1])) for i in range(len(CHUNKS[t]))]
@@ -51,11 +54,7 @@ def tile_picked_pick_lin_relu2_sub_e_kernel(tc, xT, w, b, offs, out):
         nc.sync.dma_start(w_raw[:], w.rearrange("(p j) m -> p j m", j=PACK))
         nc.sync.dma_start(bias[:], b)
 
-        nc.vector.memset(warm[:], 0.0)
-        nc.scalar.activation(warm[:], warm[:], RELU)
-
-        grouped = [keep.tile([P, SLICE, PACK], BF16, name=f"grouped{s}", align_bytes=64) for s in range(3)]
-        codes = {}
+        grouped = [keep.tile([P, PART, PACK], BF16, name=f"grouped{s}", align_bytes=64) for s in range(S // PART)]
         w_grouped = keep.tile([P, N, PACK], BF16, name="w_grouped", align_bytes=64)
         w_codes = keep.tile([P, N], U32, name="w_codes", align_bytes=64)
         w_scales = keep.tile([P, N], U8, name="w_scales", align_bytes=64)
@@ -63,32 +62,37 @@ def tile_picked_pick_lin_relu2_sub_e_kernel(tc, xT, w, b, offs, out):
         kept = keep.tile([P, S], F32, name="kept")
         result = keep.tile([P, S], F32, name="result")
 
+        def list_part(s):
+            return offsets[:, s * PART // LIST_ROWS : (s + 1) * PART // LIST_ROWS]
+
         for t in range(PACK):
             for a, z in chunks(t):
-                cut = z - (z - a) // 48 * 16 if z == T else z
+                cut = z - SCALAR_ROUNDS[t] if z == T else z
                 nc.vector.tensor_copy(rounded[t][:, a:cut], planes[t][:, a:cut])
                 if cut < z:
                     nc.scalar.activation(rounded[t][:, cut:z], planes[t][:, cut:z], COPY)
-            nc.vector.tensor_copy(grouped[0][:, :, t], planes[t][:].indirect(offsets[:, 0 : SLICE // 16]))
+            nc.vector.tensor_copy(grouped[0][:, :, t], planes[t][:].indirect(list_part(0)))
             for s in (1, 2):
-                part = offsets[:, s * SLICE // 16 : (s + 1) * SLICE // 16]
-                nc.scalar.activation(grouped[s][:, :, t], rounded[t][:].indirect(part), COPY)
+                nc.scalar.activation(grouped[s][:, :, t], rounded[t][:].indirect(list_part(s)), COPY)
 
         nc.vector.tensor_copy(w_grouped[:], w_raw[:].rearrange("p j m -> p m j"))
         nc.vector.quantize_mx(
             out=w_codes[:].bitcast(FP8X4), scales=w_scales[:], in_=w_grouped[:].rearrange("p m j -> p (m j)")
         )
 
+        codes = {}
+        sums = {}
+
         def product(c, n):
-            s, a = divmod(c, SLICE)
+            s, a = divmod(c, PART)
             if a == 0:
-                codes[s] = keep.tile([P, SLICE], U32, name=f"codes{s}", tag="codes", bufs=2, align_bytes=64)
+                codes[s] = keep.tile([P, PART], U32, name=f"codes{s}", tag="codes", bufs=2, align_bytes=64)
             nc.vector.quantize_mx(
                 out=codes[s][:, a : a + n].bitcast(FP8X4),
                 scales=scales[:, c : c + n],
                 in_=grouped[s][:].rearrange("p n j -> p (n j)")[:, PACK * a : PACK * (a + n)],
             )
-            acc = psum.tile([P, SLICE], F32, name=f"acc{c}")
+            acc = psum.tile([P, PART], F32, name=f"acc{c}")
             nc.tensor.matmul_mx(
                 out=acc[:, 0:n],
                 lhsT=w_codes[:].bitcast(FP8X4),
@@ -98,44 +102,43 @@ def tile_picked_pick_lin_relu2_sub_e_kernel(tc, xT, w, b, offs, out):
                 start=True,
                 stop=True,
             )
-            return acc[:, 0:n]
+            sums[c] = acc[:, 0:n]
 
-        def relu_s(c, n):
-            nc.scalar.activation(kept[:, c : c + n], accs[c], RELU, bias=bias[:])
+        def relu_on_scalar(c, n):
+            nc.scalar.activation(kept[:, c : c + n], sums[c], RELU, bias=bias[:])
 
-        def square_s(c, n):
+        def square_on_scalar(c, n):
             nc.scalar.activation(result[:, c : c + n], kept[:, c : c + n], SQUARE)
 
-        def relu_v(c, n):
-            nc.vector.tensor_scalar(kept[:, c : c + n], accs[c], bias[:], 0.0, ADD, MAX)
+        def relu_on_vector(c, n):
+            nc.vector.tensor_scalar(kept[:, c : c + n], sums[c], bias[:], 0.0, ADD, MAX)
 
-        def square_v(c, n):
+        def square_on_vector(c, n):
             nc.vector.tensor_tensor(result[:, c : c + n], kept[:, c : c + n], kept[:, c : c + n], MULT)
 
         def store(queue, c, n):
             queue.dma_start(out[:, c : c + n], result[:, c : c + n])
 
-        accs = {}
-        for c, n in ((0, 256), (256, 256), (512, 256), (768, 256)):
-            accs[c] = product(c, n)
-        relu_v(0, 256)
-        for c, n in ((1024, 256), (1280, 128), (1408, 128)):
-            accs[c] = product(c, n)
+        for c, n in EARLY_PIECES:
+            product(c, n)
+        relu_on_vector(0, 256)
+        for c, n in LATE_PIECES:
+            product(c, n)
 
-        relu_s(256, 256)
-        relu_s(512, 256)
-        square_s(0, 512)
+        relu_on_scalar(256, 256)
+        relu_on_scalar(512, 256)
+        square_on_scalar(0, 512)
         store(nc.sync, 0, 512)
-        relu_v(768, 256)
-        square_v(512, 256)
+        relu_on_vector(768, 256)
+        square_on_vector(512, 256)
         store(nc.sync, 512, 256)
-        relu_s(1024, 256)
-        relu_s(1280, 128)
-        relu_v(1408, 128)
-        square_v(768, 256)
+        relu_on_scalar(1024, 256)
+        relu_on_scalar(1280, 128)
+        relu_on_vector(1408, 128)
+        square_on_vector(768, 256)
         store(nc.sync, 768, 256)
-        square_s(1024, 256)
-        square_s(1280, 128)
+        square_on_scalar(1024, 256)
+        square_on_scalar(1280, 128)
         store(nc.scalar, 1024, 384)
-        square_v(1408, 128)
+        square_on_vector(1408, 128)
         store(nc.sync, 1408, 128)

@@ -27,7 +27,7 @@ CHUNKS = ((3072, 1024), (2816, 1280), (2816, 1280), (2304, 1280, 512))
 SCALAR_ROUNDS = (336, 0, 0, 0)
 
 EARLY_PIECES = ((0, 256), (256, 256), (512, 256), (768, 256))
-LATE_PIECES = ((1024, 256), (1280, 128), (1408, 128))
+LATE_PIECES = ((1024, 128), (1152, 128), (1280, 128), (1408, 128))
 
 
 def tile_picked_pick_lin_relu2_sub_e_kernel(tc, xT, w, b, offs, out):
@@ -122,23 +122,25 @@ def tile_picked_pick_lin_relu2_sub_e_kernel(tc, xT, w, b, offs, out):
         for c, n in EARLY_PIECES:
             product(c, n)
         relu_on_vector(0, 256)
+        relu_on_scalar(256, 256)
+        square_on_scalar(0, 256)
+        store(nc.sync, 0, 256)
+        relu_on_scalar(512, 256)
         for c, n in LATE_PIECES:
             product(c, n)
-
-        relu_on_scalar(256, 256)
-        relu_on_scalar(512, 256)
-        square_on_scalar(0, 512)
-        store(nc.sync, 0, 512)
+        square_on_scalar(256, 256)
+        store(nc.sync, 256, 256)
         relu_on_vector(768, 256)
-        square_on_vector(512, 256)
+        square_on_scalar(512, 256)
         store(nc.sync, 512, 256)
-        relu_on_scalar(1024, 256)
-        relu_on_scalar(1280, 128)
-        relu_on_vector(1408, 128)
-        square_on_vector(768, 256)
+        relu_on_vector(1024, 128)
+        relu_on_vector(1152, 128)
+        square_on_scalar(768, 256)
         store(nc.sync, 768, 256)
+        relu_on_vector(1280, 128)
+        relu_on_vector(1408, 128)
         square_on_scalar(1024, 256)
-        square_on_scalar(1280, 128)
-        store(nc.scalar, 1024, 384)
+        store(nc.scalar, 1024, 256)
+        square_on_vector(1280, 128)
         square_on_vector(1408, 128)
-        store(nc.sync, 1408, 128)
+        store(nc.sync, 1280, 256)

@@ -124,23 +124,20 @@ def tile_picked_pick_lin_relu2_sub_e_kernel(tc, xT, w, b, offs, out):
         relu_on_vector(0, 256)
         relu_on_scalar(256, 256)
         square_on_scalar(0, 256)
-        store(nc.sync, 0, 256)
         relu_on_scalar(512, 256)
         for c, n in LATE_PIECES:
             product(c, n)
         square_on_scalar(256, 256)
-        store(nc.sync, 256, 256)
+        store(nc.sync, 0, 512)
         relu_on_vector(768, 256)
         square_on_scalar(512, 256)
-        store(nc.sync, 512, 256)
         relu_on_vector(1024, 128)
         relu_on_vector(1152, 128)
         square_on_scalar(768, 256)
-        store(nc.sync, 768, 256)
+        store(nc.sync, 512, 512)
         relu_on_vector(1280, 128)
         relu_on_vector(1408, 128)
         square_on_scalar(1024, 256)
-        store(nc.scalar, 1024, 256)
         square_on_vector(1280, 128)
         square_on_vector(1408, 128)
-        store(nc.sync, 1280, 256)
+        store(nc.sync, 1024, 512)

@@ -23,7 +23,7 @@ ADD = mybir.AluOpType.add
 MAX = mybir.AluOpType.max
 MULT = mybir.AluOpType.mult
 
-CHUNKS = ((3072, 1024), (2816, 1280), (2816, 1280), (2304, 1280, 512))
+CHUNKS = ((3072, 1024), (2816, 1280), (2816, 1280), (2176, 1152, 512, 256))
 SCALAR_ROUNDS = (336, 0, 0, 0)
 
 EARLY_PIECES = ((0, 256), (256, 256), (512, 256), (768, 256))

@@ -24,7 +24,7 @@ MAX = mybir.AluOpType.max
 MULT = mybir.AluOpType.mult
 
 CHUNKS = ((3072, 1024), (2816, 1280), (2816, 1280), (2176, 1152, 512, 256))
-SCALAR_ROUNDS = (336, 0, 0, 0)
+SCALAR_ROUNDS = (336, 336, 336, 0)
 
 EARLY_PIECES = ((0, 256), (256, 256), (512, 256), (768, 256))
 LATE_PIECES = ((1024, 128), (1152, 128), (1280, 128), (1408, 128))

@@ -13,6 +13,7 @@ FLOPS = 2 * K * N * S
 F32 = mybir.dt.float32
 BF16 = mybir.dt.bfloat16
 U32 = mybir.dt.uint32
+I32 = mybir.dt.int32
 U16 = mybir.dt.uint16
 U8 = mybir.dt.uint8
 FP8X4 = mybir.dt.float8_e4m3fn_x4
@@ -55,6 +56,7 @@ def tile_picked_pick_lin_relu2_sub_e_kernel(tc, xT, w, b, offs, out):
         nc.sync.dma_start(bias[:], b)
 
         grouped = [keep.tile([P, PART, PACK], BF16, name=f"grouped{s}", align_bytes=64) for s in range(S // PART)]
+        pairs = keep.tile([P, 2, PART, 2], BF16, name="pairs")
         w_grouped = keep.tile([P, N, PACK], BF16, name="w_grouped", align_bytes=64)
         w_codes = keep.tile([P, N], U32, name="w_codes", align_bytes=64)
         w_scales = keep.tile([P, N], U8, name="w_scales", align_bytes=64)
@@ -71,11 +73,17 @@ def tile_picked_pick_lin_relu2_sub_e_kernel(tc, xT, w, b, offs, out):
                 nc.vector.tensor_copy(rounded[t][:, a:cut], planes[t][:, a:cut])
                 if cut < z:
                     nc.scalar.activation(rounded[t][:, cut:z], planes[t][:, cut:z], COPY)
-            nc.vector.tensor_copy(grouped[0][:, :, t], planes[t][:].indirect(list_part(0)))
+            nc.vector.tensor_copy(pairs[:, t // 2, :, t % 2], planes[t][:].indirect(list_part(0)))
             for s in (1, 2):
                 nc.scalar.activation(grouped[s][:, :, t], rounded[t][:].indirect(list_part(s)), COPY)
 
         nc.vector.tensor_copy(w_grouped[:], w_raw[:].rearrange("p j m -> p m j"))
+        pair_words = pairs[:].rearrange("p u n e -> p u (n e)").bitcast(I32)
+        for a in (0, PART // 2):
+            nc.vector.tensor_copy(
+                grouped[0][:, a : a + PART // 2, :].bitcast(I32),
+                pair_words[:, :, a : a + PART // 2].rearrange("p u n -> p n u"),
+            )
         nc.vector.quantize_mx(
             out=w_codes[:].bitcast(FP8X4), scales=w_scales[:], in_=w_grouped[:].rearrange("p m j -> p (m j)")
         )

@@ -12,8 +12,8 @@ FLOPS = 2 * K * N * S
 
 F32 = mybir.dt.float32
 BF16 = mybir.dt.bfloat16
-U32 = mybir.dt.uint32
 I32 = mybir.dt.int32
+U32 = mybir.dt.uint32
 U16 = mybir.dt.uint16
 U8 = mybir.dt.uint8
 FP8X4 = mybir.dt.float8_e4m3fn_x4
@@ -26,9 +26,7 @@ MULT = mybir.AluOpType.mult
 
 CHUNKS = ((3072, 1024), (2816, 1280), (2816, 1280), (2176, 1152, 512, 256))
 SCALAR_ROUNDS = (336, 336, 336, 0)
-
-EARLY_PIECES = ((0, 256), (256, 256), (512, 256), (768, 256))
-LATE_PIECES = ((1024, 128), (1152, 128), (1280, 128), (1408, 128))
+PIECES = ((0, 256), (256, 256), (512, 256), (768, 256), (1024, 128), (1152, 128), (1280, 128), (1408, 128))
 
 
 def tile_picked_pick_lin_relu2_sub_e_kernel(tc, xT, w, b, offs, out):
@@ -55,11 +53,12 @@ def tile_picked_pick_lin_relu2_sub_e_kernel(tc, xT, w, b, offs, out):
         nc.sync.dma_start(w_raw[:], w.rearrange("(p j) m -> p j m", j=PACK))
         nc.sync.dma_start(bias[:], b)
 
-        grouped = [keep.tile([P, PART, PACK], BF16, name=f"grouped{s}", align_bytes=64) for s in range(S // PART)]
+        grouped = [keep.tile([P, PART, PACK], BF16, name=f"grouped{s}", tag=f"grouped{s}", align_bytes=64) for s in (0, 1)]
         pairs = keep.tile([P, 2, PART, 2], BF16, name="pairs")
         w_grouped = keep.tile([P, N, PACK], BF16, name="w_grouped", align_bytes=64)
         w_codes = keep.tile([P, N], U32, name="w_codes", align_bytes=64)
         w_scales = keep.tile([P, N], U8, name="w_scales", align_bytes=64)
+        codes = keep.tile([P, S], U32, name="codes", align_bytes=64)
         scales = keep.tile([P, S], U8, name="scales", align_bytes=64)
         kept = keep.tile([P, S], F32, name="kept")
         result = keep.tile([P, S], F32, name="result")
@@ -73,30 +72,21 @@ def tile_picked_pick_lin_relu2_sub_e_kernel(tc, xT, w, b, offs, out):
                 nc.vector.tensor_copy(rounded[t][:, a:cut], planes[t][:, a:cut])
                 if cut < z:
                     nc.scalar.activation(rounded[t][:, cut:z], planes[t][:, cut:z], COPY)
-            nc.vector.tensor_copy(pairs[:, t // 2, :, t % 2], planes[t][:].indirect(list_part(0)))
-            for s in (1, 2):
-                nc.scalar.activation(grouped[s][:, :, t], rounded[t][:].indirect(list_part(s)), COPY)
+            nc.vector.tensor_copy(grouped[0][:, :, t], planes[t][:].indirect(list_part(0)))
+            nc.scalar.activation(grouped[1][:, :, t], rounded[t][:].indirect(list_part(1)), COPY)
+            nc.scalar.activation(pairs[:, t // 2, :, t % 2], rounded[t][:].indirect(list_part(2)), COPY)
 
         nc.vector.tensor_copy(w_grouped[:], w_raw[:].rearrange("p j m -> p m j"))
-        pair_words = pairs[:].rearrange("p u n e -> p u (n e)").bitcast(I32)
-        for a in (0, PART // 2):
-            nc.vector.tensor_copy(
-                grouped[0][:, a : a + PART // 2, :].bitcast(I32),
-                pair_words[:, :, a : a + PART // 2].rearrange("p u n -> p n u"),
-            )
         nc.vector.quantize_mx(
             out=w_codes[:].bitcast(FP8X4), scales=w_scales[:], in_=w_grouped[:].rearrange("p m j -> p (m j)")
         )
 
-        codes = {}
         sums = {}
 
         def product(c, n):
             s, a = divmod(c, PART)
-            if a == 0:
-                codes[s] = keep.tile([P, PART], U32, name=f"codes{s}", tag="codes", bufs=2, align_bytes=64)
             nc.vector.quantize_mx(
-                out=codes[s][:, a : a + n].bitcast(FP8X4),
+                out=codes[:, c : c + n].bitcast(FP8X4),
                 scales=scales[:, c : c + n],
                 in_=grouped[s][:].rearrange("p n j -> p (n j)")[:, PACK * a : PACK * (a + n)],
             )
@@ -105,7 +95,7 @@ def tile_picked_pick_lin_relu2_sub_e_kernel(tc, xT, w, b, offs, out):
                 out=acc[:, 0:n],
                 lhsT=w_codes[:].bitcast(FP8X4),
                 lhsT_scale=w_scales[:],
-                rhs=codes[s][:, a : a + n].bitcast(FP8X4),
+                rhs=codes[:, c : c + n].bitcast(FP8X4),
                 rhs_scale=scales[:, c : c + n],
                 start=True,
                 stop=True,
@@ -124,28 +114,37 @@ def tile_picked_pick_lin_relu2_sub_e_kernel(tc, xT, w, b, offs, out):
         def square_on_vector(c, n):
             nc.vector.tensor_tensor(result[:, c : c + n], kept[:, c : c + n], kept[:, c : c + n], MULT)
 
-        def store(queue, c, n):
-            queue.dma_start(out[:, c : c + n], result[:, c : c + n])
+        def store(c, n):
+            nc.sync.dma_start(out[:, c : c + n], result[:, c : c + n])
 
-        for c, n in EARLY_PIECES:
+        for c, n in PIECES[:4]:
             product(c, n)
-        relu_on_vector(0, 256)
+
+        grouped.append(keep.tile([P, PART, PACK], BF16, name="grouped2", tag="grouped0", align_bytes=64))
+        pair_words = pairs[:].rearrange("p u n e -> p u (n e)").bitcast(I32)
+        for a in (0, PART // 2):
+            nc.vector.tensor_copy(
+                grouped[2][:, a : a + PART // 2, :].bitcast(I32),
+                pair_words[:, :, a : a + PART // 2].rearrange("p u n -> p n u"),
+            )
+        for c, n in PIECES[4:]:
+            product(c, n)
+
+        relu_on_scalar(0, 256)
         relu_on_scalar(256, 256)
-        square_on_scalar(0, 256)
         relu_on_scalar(512, 256)
-        for c, n in LATE_PIECES:
-            product(c, n)
-        square_on_scalar(256, 256)
-        store(nc.sync, 0, 512)
+        square_on_scalar(0, 384)
+        store(0, 384)
+        square_on_scalar(384, 384)
         relu_on_vector(768, 256)
-        square_on_scalar(512, 256)
-        relu_on_vector(1024, 128)
+        relu_on_scalar(1024, 128)
+        square_on_scalar(768, 128)
+        store(384, 512)
         relu_on_vector(1152, 128)
-        square_on_scalar(768, 256)
-        store(nc.sync, 512, 512)
         relu_on_vector(1280, 128)
         relu_on_vector(1408, 128)
-        square_on_scalar(1024, 256)
-        square_on_vector(1280, 128)
+        square_on_scalar(896, 256)
+        square_on_vector(1152, 128)
+        square_on_scalar(1280, 128)
         square_on_vector(1408, 128)
-        store(nc.sync, 1024, 512)
+        store(896, 640)

@@ -24,8 +24,8 @@ ADD = mybir.AluOpType.add
 MAX = mybir.AluOpType.max
 MULT = mybir.AluOpType.mult
 
-CHUNKS = ((3072, 1024), (2816, 1280), (2816, 1280), (2176, 1152, 512, 256))
-SCALAR_ROUNDS = (336, 336, 336, 0)
+CHUNKS = ((4096,), (4096,), (2816, 1280), (2176, 1152, 512, 256))
+SCALAR_ROUNDS = ((1360,), (1280,), (0, 512), (0, 384, 0, 0))
 PIECES = ((0, 256), (256, 256), (512, 256), (768, 256), (1024, 128), (1152, 128), (1280, 128), (1408, 128))
 
 
@@ -67,8 +67,8 @@ def tile_picked_pick_lin_relu2_sub_e_kernel(tc, xT, w, b, offs, out):
             return offsets[:, s * PART // LIST_ROWS : (s + 1) * PART // LIST_ROWS]
 
         for t in range(PACK):
-            for a, z in chunks(t):
-                cut = z - SCALAR_ROUNDS[t] if z == T else z
+            for (a, z), share in zip(chunks(t), SCALAR_ROUNDS[t]):
+                cut = z - share
                 nc.vector.tensor_copy(rounded[t][:, a:cut], planes[t][:, a:cut])
                 if cut < z:
                     nc.scalar.activation(rounded[t][:, cut:z], planes[t][:, cut:z], COPY)
@@ -132,19 +132,21 @@ def tile_picked_pick_lin_relu2_sub_e_kernel(tc, xT, w, b, offs, out):
 
         relu_on_scalar(0, 256)
         relu_on_scalar(256, 256)
+        square_on_scalar(0, 256)
+        store(0, 256)
         relu_on_scalar(512, 256)
-        square_on_scalar(0, 384)
-        store(0, 384)
-        square_on_scalar(384, 384)
+        square_on_scalar(256, 256)
+        store(256, 256)
+        square_on_scalar(512, 256)
+        store(512, 256)
         relu_on_vector(768, 256)
         relu_on_scalar(1024, 128)
-        square_on_scalar(768, 128)
-        store(384, 512)
+        square_on_scalar(768, 256)
+        store(768, 256)
         relu_on_vector(1152, 128)
         relu_on_vector(1280, 128)
         relu_on_vector(1408, 128)
-        square_on_scalar(896, 256)
-        square_on_vector(1152, 128)
+        square_on_vector(1024, 256)
         square_on_scalar(1280, 128)
-        square_on_vector(1408, 128)
-        store(896, 640)
+        square_on_scalar(1408, 128)
+        store(1024, 512)

@@ -24,8 +24,8 @@ ADD = mybir.AluOpType.add
 MAX = mybir.AluOpType.max
 MULT = mybir.AluOpType.mult
 
-CHUNKS = ((4096,), (4096,), (2816, 1280), (2176, 1152, 512, 256))
-SCALAR_ROUNDS = ((1360,), (1280,), (0, 512), (0, 384, 0, 0))
+LAST_CHUNKS = (2560, 1152, 384)
+SCALAR_ROUNDS = (1184, 384, 128)
 PIECES = ((0, 256), (256, 256), (512, 256), (768, 256), (1024, 128), (1152, 128), (1280, 128), (1408, 128))
 
 
@@ -37,24 +37,25 @@ def tile_picked_pick_lin_relu2_sub_e_kernel(tc, xT, w, b, offs, out):
 
         offsets = keep.tile([P, S // LIST_ROWS], U16, name="offsets")
         planes = [keep.tile([P, T], F32, name=f"plane{t}") for t in range(PACK)]
-        rounded = [keep.tile([P, T], BF16, name=f"rounded{t}") for t in range(PACK)]
+        rounded = keep.tile([P, T], BF16, name="rounded")
         w_raw = keep.tile([P, PACK, N], F32, name="w_raw")
         bias = keep.tile([P, 1], F32, name="bias")
 
-        def chunks(t):
-            return [(sum(CHUNKS[t][:i]), sum(CHUNKS[t][: i + 1])) for i in range(len(CHUNKS[t]))]
-
+        chunks = [(sum(LAST_CHUNKS[:i]), sum(LAST_CHUNKS[: i + 1])) for i in range(len(LAST_CHUNKS))]
         x_rows = xT.rearrange("(p j) n -> p j n", j=PACK)
-        for t in range(PACK):
-            for a, z in chunks(t):
-                nc.sync.dma_start(planes[t][:, a:z], x_rows[:, t, a:z])
-                if (t, a) == (0, 0):
-                    nc.sync.dma_start(offsets[:], offs)
+        nc.sync.dma_start(planes[0][:], x_rows[:, 0, :])
+        nc.sync.dma_start(offsets[:], offs)
+        nc.sync.dma_start(planes[1][:], x_rows[:, 1, :])
+        nc.sync.dma_start(planes[2][:], x_rows[:, 2, :])
+        for a, z in chunks:
+            nc.sync.dma_start(planes[3][:, a:z], x_rows[:, 3, a:z])
         nc.sync.dma_start(w_raw[:], w.rearrange("(p j) m -> p j m", j=PACK))
         nc.sync.dma_start(bias[:], b)
 
         grouped = [keep.tile([P, PART, PACK], BF16, name=f"grouped{s}", tag=f"grouped{s}", align_bytes=64) for s in (0, 1)]
         pairs = keep.tile([P, 2, PART, 2], BF16, name="pairs")
+        middle = [keep.tile([P, PART], BF16, name=f"middle{t}") for t in range(PACK - 1)]
+        last = keep.tile([P, PACK - 1, PART], BF16, name="last")
         w_grouped = keep.tile([P, N, PACK], BF16, name="w_grouped", align_bytes=64)
         w_codes = keep.tile([P, N], U32, name="w_codes", align_bytes=64)
         w_scales = keep.tile([P, N], U8, name="w_scales", align_bytes=64)
@@ -66,15 +67,23 @@ def tile_picked_pick_lin_relu2_sub_e_kernel(tc, xT, w, b, offs, out):
         def list_part(s):
             return offsets[:, s * PART // LIST_ROWS : (s + 1) * PART // LIST_ROWS]
 
-        for t in range(PACK):
-            for (a, z), share in zip(chunks(t), SCALAR_ROUNDS[t]):
-                cut = z - share
-                nc.vector.tensor_copy(rounded[t][:, a:cut], planes[t][:, a:cut])
-                if cut < z:
-                    nc.scalar.activation(rounded[t][:, cut:z], planes[t][:, cut:z], COPY)
+        for t in range(PACK - 1):
             nc.vector.tensor_copy(grouped[0][:, :, t], planes[t][:].indirect(list_part(0)))
-            nc.scalar.activation(grouped[1][:, :, t], rounded[t][:].indirect(list_part(1)), COPY)
-            nc.scalar.activation(pairs[:, t // 2, :, t % 2], rounded[t][:].indirect(list_part(2)), COPY)
+            nc.scalar.activation(middle[t][:], planes[t][:].indirect(list_part(1)), COPY)
+            nc.scalar.activation(last[:, t, :], planes[t][:].indirect(list_part(2)), COPY)
+            nc.vector.tensor_copy(grouped[1][:, :, t], middle[t][:])
+            if t == 1:
+                nc.vector.tensor_copy(pairs[:, 0, :, :], last[:, 0:2, :].rearrange("p e n -> p n e"))
+            if t == 2:
+                nc.vector.tensor_copy(pairs[:, 1, :, 0], last[:, 2, :])
+
+        for (a, z), share in zip(chunks, SCALAR_ROUNDS):
+            cut = z - share
+            nc.vector.tensor_copy(rounded[:, a:cut], planes[3][:, a:cut])
+            nc.scalar.activation(rounded[:, cut:z], planes[3][:, cut:z], COPY)
+        nc.vector.tensor_copy(grouped[0][:, :, 3], planes[3][:].indirect(list_part(0)))
+        nc.scalar.activation(grouped[1][:, :, 3], rounded[:].indirect(list_part(1)), COPY)
+        nc.scalar.activation(pairs[:, 1, :, 1], rounded[:].indirect(list_part(2)), COPY)
 
         nc.vector.tensor_copy(w_grouped[:], w_raw[:].rearrange("p j m -> p m j"))
         nc.vector.quantize_mx(
@@ -133,7 +142,9 @@ def tile_picked_pick_lin_relu2_sub_e_kernel(tc, xT, w, b, offs, out):
         relu_on_scalar(0, 256)
         relu_on_scalar(256, 256)
         square_on_scalar(0, 256)
-        store(0, 256)
+        store(0, 64)
+        store(64, 64)
+        store(128, 128)
         relu_on_scalar(512, 256)
         square_on_scalar(256, 256)
         store(256, 256)

@@ -50,7 +50,8 @@ def tile_picked_pick_lin_relu2_sub_e_kernel(tc, xT, w, b, offs, out):
         for a, z in chunks:
             nc.sync.dma_start(planes[3][:, a:z], x_rows[:, 3, a:z])
         nc.sync.dma_start(w_raw[:], w.rearrange("(p j) m -> p j m", j=PACK))
-        nc.sync.dma_start(bias[:], b)
+        for a in (0, P // 2):
+            nc.sync.dma_start(bias[a : a + P // 2, :], b[a : a + P // 2, :])
 
         grouped = [keep.tile([P, PART, PACK], BF16, name=f"grouped{s}", tag=f"grouped{s}", align_bytes=64) for s in (0, 1)]
         pairs = keep.tile([P, 2, PART, 2], BF16, name="pairs")
@@ -142,8 +143,7 @@ def tile_picked_pick_lin_relu2_sub_e_kernel(tc, xT, w, b, offs, out):
         relu_on_scalar(0, 256)
         relu_on_scalar(256, 256)
         square_on_scalar(0, 256)
-        store(0, 64)
-        store(64, 64)
+        store(0, 128)
         store(128, 128)
         relu_on_scalar(512, 256)
         square_on_scalar(256, 256)

@@ -24,8 +24,8 @@ ADD = mybir.AluOpType.add
 MAX = mybir.AluOpType.max
 MULT = mybir.AluOpType.mult
 
-LAST_CHUNKS = (2560, 1152, 384)
-SCALAR_ROUNDS = (1184, 384, 128)
+LAST_CHUNKS = (2688, 1024, 384)
+SCALAR_ROUNDS = (1056, 336, 128)
 PIECES = ((0, 256), (256, 256), (512, 256), (768, 256), (1024, 128), (1152, 128), (1280, 128), (1408, 128))
 
 
@@ -71,12 +71,15 @@ def tile_picked_pick_lin_relu2_sub_e_kernel(tc, xT, w, b, offs, out):
         for t in range(PACK - 1):
             nc.vector.tensor_copy(grouped[0][:, :, t], planes[t][:].indirect(list_part(0)))
             nc.scalar.activation(middle[t][:], planes[t][:].indirect(list_part(1)), COPY)
-            nc.scalar.activation(last[:, t, :], planes[t][:].indirect(list_part(2)), COPY)
+            for a in (0, PART // 2):
+                half = offsets[:, (2 * PART + a) // LIST_ROWS : (2 * PART + a + PART // 2) // LIST_ROWS]
+                nc.scalar.activation(last[:, t, a : a + PART // 2], planes[t][:].indirect(half), COPY)
             nc.vector.tensor_copy(grouped[1][:, :, t], middle[t][:])
             if t == 1:
                 nc.vector.tensor_copy(pairs[:, 0, :, :], last[:, 0:2, :].rearrange("p e n -> p n e"))
             if t == 2:
-                nc.vector.tensor_copy(pairs[:, 1, :, 0], last[:, 2, :])
+                for a in (0, PART // 2):
+                    nc.vector.tensor_copy(pairs[:, 1, a : a + PART // 2, 0], last[:, 2, a : a + PART // 2])
 
         for (a, z), share in zip(chunks, SCALAR_ROUNDS):
             cut = z - share

@@ -50,8 +50,7 @@ def tile_picked_pick_lin_relu2_sub_e_kernel(tc, xT, w, b, offs, out):
         for a, z in chunks:
             nc.sync.dma_start(planes[3][:, a:z], x_rows[:, 3, a:z])
         nc.sync.dma_start(w_raw[:], w.rearrange("(p j) m -> p j m", j=PACK))
-        for a in (0, P // 2):
-            nc.sync.dma_start(bias[a : a + P // 2, :], b[a : a + P // 2, :])
+        nc.sync.dma_start(bias[:], b)
 
         grouped = [keep.tile([P, PART, PACK], BF16, name=f"grouped{s}", tag=f"grouped{s}", align_bytes=64) for s in (0, 1)]
         pairs = keep.tile([P, 2, PART, 2], BF16, name="pairs")
@@ -161,6 +160,7 @@ def tile_picked_pick_lin_relu2_sub_e_kernel(tc, xT, w, b, offs, out):
         relu_on_vector(1280, 128)
         relu_on_vector(1408, 128)
         square_on_vector(1024, 256)
+        store(1024, 256)
         square_on_scalar(1280, 128)
         square_on_scalar(1408, 128)
-        store(1024, 512)
+        store(1280, 256)

@@ -152,15 +152,12 @@ def tile_picked_pick_lin_relu2_sub_e_kernel(tc, xT, w, b, offs, out):
         store(256, 256)
         square_on_scalar(512, 256)
         store(512, 256)
-        relu_on_vector(768, 256)
-        relu_on_scalar(1024, 128)
+        for c, n in PIECES[3:]:
+            relu_on_vector(c, n)
         square_on_scalar(768, 256)
         store(768, 256)
-        relu_on_vector(1152, 128)
-        relu_on_vector(1280, 128)
-        relu_on_vector(1408, 128)
-        square_on_vector(1024, 256)
+        square_on_scalar(1024, 256)
         store(1024, 256)
-        square_on_scalar(1280, 128)
-        square_on_scalar(1408, 128)
+        square_on_vector(1280, 128)
+        square_on_vector(1408, 128)
         store(1280, 256)

@@ -6,7 +6,9 @@ K, T, S, N = 512, 4096, 1536, 128
 P = 128
 PACK = 4
 PART = 512
+HALF = PART // 2
 LIST_ROWS = 16
+BANK = 512
 
 FLOPS = 2 * K * N * S
 
@@ -26,7 +28,8 @@ MULT = mybir.AluOpType.mult
 
 LAST_CHUNKS = (2688, 1024, 384)
 SCALAR_ROUNDS = (1056, 336, 128)
-PIECES = ((0, 256), (256, 256), (512, 256), (768, 256), (1024, 128), (1152, 128), (1280, 128), (1408, 128))
+WIDE, NARROW = 256, 128
+PIECES = tuple((c, WIDE) for c in range(0, 2 * PART, WIDE)) + tuple((c, NARROW) for c in range(2 * PART, S, NARROW))
 
 
 def tile_picked_pick_lin_relu2_sub_e_kernel(tc, xT, w, b, offs, out):
@@ -54,8 +57,8 @@ def tile_picked_pick_lin_relu2_sub_e_kernel(tc, xT, w, b, offs, out):
 
         grouped = [keep.tile([P, PART, PACK], BF16, name=f"grouped{s}", tag=f"grouped{s}", align_bytes=64) for s in (0, 1)]
         pairs = keep.tile([P, 2, PART, 2], BF16, name="pairs")
-        middle = [keep.tile([P, PART], BF16, name=f"middle{t}") for t in range(PACK - 1)]
-        last = keep.tile([P, PACK - 1, PART], BF16, name="last")
+        flat1 = [keep.tile([P, PART], BF16, name=f"flat1_{t}") for t in range(PACK - 1)]
+        flat2 = keep.tile([P, PACK - 1, PART], BF16, name="flat2")
         w_grouped = keep.tile([P, N, PACK], BF16, name="w_grouped", align_bytes=64)
         w_codes = keep.tile([P, N], U32, name="w_codes", align_bytes=64)
         w_scales = keep.tile([P, N], U8, name="w_scales", align_bytes=64)
@@ -64,29 +67,28 @@ def tile_picked_pick_lin_relu2_sub_e_kernel(tc, xT, w, b, offs, out):
         kept = keep.tile([P, S], F32, name="kept")
         result = keep.tile([P, S], F32, name="result")
 
-        def list_part(s):
-            return offsets[:, s * PART // LIST_ROWS : (s + 1) * PART // LIST_ROWS]
+        def entries(c, n):
+            return offsets[:, c // LIST_ROWS : (c + n) // LIST_ROWS]
 
         for t in range(PACK - 1):
-            nc.vector.tensor_copy(grouped[0][:, :, t], planes[t][:].indirect(list_part(0)))
-            nc.scalar.activation(middle[t][:], planes[t][:].indirect(list_part(1)), COPY)
-            for a in (0, PART // 2):
-                half = offsets[:, (2 * PART + a) // LIST_ROWS : (2 * PART + a + PART // 2) // LIST_ROWS]
-                nc.scalar.activation(last[:, t, a : a + PART // 2], planes[t][:].indirect(half), COPY)
-            nc.vector.tensor_copy(grouped[1][:, :, t], middle[t][:])
+            nc.vector.tensor_copy(grouped[0][:, :, t], planes[t][:].indirect(entries(0, PART)))
+            nc.scalar.activation(flat1[t][:], planes[t][:].indirect(entries(PART, PART)), COPY)
+            for a in (0, HALF):
+                nc.scalar.activation(flat2[:, t, a : a + HALF], planes[t][:].indirect(entries(2 * PART + a, HALF)), COPY)
+            nc.vector.tensor_copy(grouped[1][:, :, t], flat1[t][:])
             if t == 1:
-                nc.vector.tensor_copy(pairs[:, 0, :, :], last[:, 0:2, :].rearrange("p e n -> p n e"))
+                nc.vector.tensor_copy(pairs[:, 0, :, :], flat2[:, 0:2, :].rearrange("p e n -> p n e"))
             if t == 2:
-                for a in (0, PART // 2):
-                    nc.vector.tensor_copy(pairs[:, 1, a : a + PART // 2, 0], last[:, 2, a : a + PART // 2])
+                for a in (0, HALF):
+                    nc.vector.tensor_copy(pairs[:, 1, a : a + HALF, 0], flat2[:, 2, a : a + HALF])
 
         for (a, z), share in zip(chunks, SCALAR_ROUNDS):
             cut = z - share
             nc.vector.tensor_copy(rounded[:, a:cut], planes[3][:, a:cut])
             nc.scalar.activation(rounded[:, cut:z], planes[3][:, cut:z], COPY)
-        nc.vector.tensor_copy(grouped[0][:, :, 3], planes[3][:].indirect(list_part(0)))
-        nc.scalar.activation(grouped[1][:, :, 3], rounded[:].indirect(list_part(1)), COPY)
-        nc.scalar.activation(pairs[:, 1, :, 1], rounded[:].indirect(list_part(2)), COPY)
+        nc.vector.tensor_copy(grouped[0][:, :, 3], planes[3][:].indirect(entries(0, PART)))
+        nc.scalar.activation(grouped[1][:, :, 3], rounded[:].indirect(entries(PART, PART)), COPY)
+        nc.scalar.activation(pairs[:, 1, :, 1], rounded[:].indirect(entries(2 * PART, PART)), COPY)
 
         nc.vector.tensor_copy(w_grouped[:], w_raw[:].rearrange("p j m -> p m j"))
         nc.vector.quantize_mx(
@@ -102,7 +104,7 @@ def tile_picked_pick_lin_relu2_sub_e_kernel(tc, xT, w, b, offs, out):
                 scales=scales[:, c : c + n],
                 in_=grouped[s][:].rearrange("p n j -> p (n j)")[:, PACK * a : PACK * (a + n)],
             )
-            acc = psum.tile([P, PART], F32, name=f"acc{c}")
+            acc = psum.tile([P, BANK], F32, name=f"acc{c}")
             nc.tensor.matmul_mx(
                 out=acc[:, 0:n],
                 lhsT=w_codes[:].bitcast(FP8X4),
@@ -126,38 +128,35 @@ def tile_picked_pick_lin_relu2_sub_e_kernel(tc, xT, w, b, offs, out):
         def square_on_vector(c, n):
             nc.vector.tensor_tensor(result[:, c : c + n], kept[:, c : c + n], kept[:, c : c + n], MULT)
 
-        def store(c, n):
-            nc.sync.dma_start(out[:, c : c + n], result[:, c : c + n])
+        def store(c):
+            nc.sync.dma_start(out[:, c : c + WIDE], result[:, c : c + WIDE])
 
-        for c, n in PIECES[:4]:
+        wide_pieces = 2 * PART // WIDE
+        for c, n in PIECES[:wide_pieces]:
             product(c, n)
 
         grouped.append(keep.tile([P, PART, PACK], BF16, name="grouped2", tag="grouped0", align_bytes=64))
         pair_words = pairs[:].rearrange("p u n e -> p u (n e)").bitcast(I32)
-        for a in (0, PART // 2):
+        for a in (0, HALF):
             nc.vector.tensor_copy(
-                grouped[2][:, a : a + PART // 2, :].bitcast(I32),
-                pair_words[:, :, a : a + PART // 2].rearrange("p u n -> p n u"),
+                grouped[2][:, a : a + HALF, :].bitcast(I32),
+                pair_words[:, :, a : a + HALF].rearrange("p u n -> p n u"),
             )
-        for c, n in PIECES[4:]:
+        for c, n in PIECES[wide_pieces:]:
             product(c, n)
 
-        relu_on_scalar(0, 256)
-        relu_on_scalar(256, 256)
-        square_on_scalar(0, 256)
-        store(0, 128)
-        store(128, 128)
-        relu_on_scalar(512, 256)
-        square_on_scalar(256, 256)
-        store(256, 256)
-        square_on_scalar(512, 256)
-        store(512, 256)
-        for c, n in PIECES[3:]:
+        alone = wide_pieces - 1
+        relu_on_scalar(0, WIDE)
+        for i in range(alone):
+            if i + 1 < alone:
+                relu_on_scalar((i + 1) * WIDE, WIDE)
+            square_on_scalar(i * WIDE, WIDE)
+            store(i * WIDE)
+        for c, n in PIECES[alone:]:
             relu_on_vector(c, n)
-        square_on_scalar(768, 256)
-        store(768, 256)
-        square_on_scalar(1024, 256)
-        store(1024, 256)
-        square_on_vector(1280, 128)
-        square_on_vector(1408, 128)
-        store(1280, 256)
+        for c in range(alone * WIDE, S - WIDE, WIDE):
+            square_on_scalar(c, WIDE)
+            store(c)
+        for c, n in PIECES[-2:]:
+            square_on_vector(c, n)
+        store(S - WIDE)

@@ -114,16 +114,17 @@ def tile_picked_pick_lin_relu2_sub_e_kernel(tc, xT, w, b, offs, out):
                 start=True,
                 stop=True,
             )
-            sums[c] = acc[:, 0:n]
+            for a in range(0, n, NARROW):
+                sums[c + a] = acc[:, a:n]
 
         def relu_on_scalar(c, n):
-            nc.scalar.activation(kept[:, c : c + n], sums[c], RELU, bias=bias[:])
+            nc.scalar.activation(kept[:, c : c + n], sums[c][:, 0:n], RELU, bias=bias[:])
 
         def square_on_scalar(c, n):
             nc.scalar.activation(result[:, c : c + n], kept[:, c : c + n], SQUARE)
 
         def relu_on_vector(c, n):
-            nc.vector.tensor_scalar(kept[:, c : c + n], sums[c], bias[:], 0.0, ADD, MAX)
+            nc.vector.tensor_scalar(kept[:, c : c + n], sums[c][:, 0:n], bias[:], 0.0, ADD, MAX)
 
         def square_on_vector(c, n):
             nc.vector.tensor_tensor(result[:, c : c + n], kept[:, c : c + n], kept[:, c : c + n], MULT)
@@ -152,10 +153,11 @@ def tile_picked_pick_lin_relu2_sub_e_kernel(tc, xT, w, b, offs, out):
                 relu_on_scalar((i + 1) * WIDE, WIDE)
             square_on_scalar(i * WIDE, WIDE)
             store(i * WIDE)
-        for c, n in PIECES[alone:]:
-            relu_on_vector(c, n)
+        for c in range(alone * WIDE, S, NARROW):
+            relu_on_vector(c, NARROW)
         for c in range(alone * WIDE, S - WIDE, WIDE):
-            square_on_scalar(c, WIDE)
+            square_on_scalar(c, NARROW)
+            square_on_scalar(c + NARROW, NARROW)
             store(c)
         for c, n in PIECES[-2:]:
             square_on_vector(c, n)

@@ -46,8 +46,9 @@ def tile_picked_pick_lin_relu2_sub_e_kernel(tc, xT, w, b, offs, out):
 
         chunks = [(sum(LAST_CHUNKS[:i]), sum(LAST_CHUNKS[: i + 1])) for i in range(len(LAST_CHUNKS))]
         x_rows = xT.rearrange("(p j) n -> p j n", j=PACK)
-        nc.sync.dma_start(planes[0][:], x_rows[:, 0, :])
+        nc.scalar.dma_start(planes[0][:, 0 : T // 2], x_rows[:, 0, 0 : T // 2])
         nc.sync.dma_start(offsets[:], offs)
+        nc.sync.dma_start(planes[0][:, T // 2 : T], x_rows[:, 0, T // 2 : T])
         nc.sync.dma_start(planes[1][:], x_rows[:, 1, :])
         nc.sync.dma_start(planes[2][:], x_rows[:, 2, :])
         for a, z in chunks:

from contextlib import ExitStack

import concourse.mybir as mybir

K, T, S, N = 512, 4096, 1536, 128
P = 128
PACK = 4
PART = 512
HALF = PART // 2
LIST_ROWS = 16
BANK = 512

FLOPS = 2 * K * N * S

F32 = mybir.dt.float32
BF16 = mybir.dt.bfloat16
I32 = mybir.dt.int32
U32 = mybir.dt.uint32
U16 = mybir.dt.uint16
U8 = mybir.dt.uint8
FP8X4 = mybir.dt.float8_e4m3fn_x4
COPY = mybir.ActivationFunctionType.Copy
RELU = mybir.ActivationFunctionType.Relu
SQUARE = mybir.ActivationFunctionType.Square
ADD = mybir.AluOpType.add
MAX = mybir.AluOpType.max
MULT = mybir.AluOpType.mult

LAST_CHUNKS = (2688, 1024, 384)
SCALAR_ROUNDS = (1056, 336, 128)
WIDE, NARROW = 256, 128
PIECES = tuple((c, WIDE) for c in range(0, 2 * PART, WIDE)) + tuple((c, NARROW) for c in range(2 * PART, S, NARROW))


def tile_picked_pick_lin_relu2_sub_e_kernel(tc, xT, w, b, offs, out):
    nc = tc.nc
    with ExitStack() as ctx:
        keep = ctx.enter_context(tc.tile_pool(name="keep", bufs=1))
        psum = ctx.enter_context(tc.psum_pool(name="psum", bufs=1))

        offsets = keep.tile([P, S // LIST_ROWS], U16, name="offsets")
        planes = [keep.tile([P, T], F32, name=f"plane{t}") for t in range(PACK)]
        rounded = keep.tile([P, T], BF16, name="rounded")
        w_raw = keep.tile([P, PACK, N], F32, name="w_raw")
        bias = keep.tile([P, 1], F32, name="bias")

        chunks = [(sum(LAST_CHUNKS[:i]), sum(LAST_CHUNKS[: i + 1])) for i in range(len(LAST_CHUNKS))]
        x_rows = xT.rearrange("(p j) n -> p j n", j=PACK)
        nc.scalar.dma_start(planes[0][:, 0 : T // 2], x_rows[:, 0, 0 : T // 2])
        nc.sync.dma_start(offsets[:], offs)
        nc.sync.dma_start(planes[0][:, T // 2 : T], x_rows[:, 0, T // 2 : T])
        nc.sync.dma_start(planes[1][:], x_rows[:, 1, :])
        nc.sync.dma_start(planes[2][:], x_rows[:, 2, :])
        for a, z in chunks:
            nc.sync.dma_start(planes[3][:, a:z], x_rows[:, 3, a:z])
        nc.sync.dma_start(w_raw[:], w.rearrange("(p j) m -> p j m", j=PACK))
        nc.sync.dma_start(bias[:], b)

        grouped = [keep.tile([P, PART, PACK], BF16, name=f"grouped{s}", tag=f"grouped{s}", align_bytes=64) for s in (0, 1)]
        pairs = keep.tile([P, 2, PART, 2], BF16, name="pairs")
        flat1 = [keep.tile([P, PART], BF16, name=f"flat1_{t}") for t in range(PACK - 1)]
        flat2 = keep.tile([P, PACK - 1, PART], BF16, name="flat2")
        w_grouped = keep.tile([P, N, PACK], BF16, name="w_grouped", align_bytes=64)
        w_codes = keep.tile([P, N], U32, name="w_codes", align_bytes=64)
        w_scales = keep.tile([P, N], U8, name="w_scales", align_bytes=64)
        codes = keep.tile([P, S], U32, name="codes", align_bytes=64)
        scales = keep.tile([P, S], U8, name="scales", align_bytes=64)
        kept = keep.tile([P, S], F32, name="kept")
        result = keep.tile([P, S], F32, name="result")

        def entries(c, n):
            return offsets[:, c // LIST_ROWS : (c + n) // LIST_ROWS]

        for t in range(PACK - 1):
            nc.vector.tensor_copy(grouped[0][:, :, t], planes[t][:].indirect(entries(0, PART)))
            nc.scalar.activation(flat1[t][:], planes[t][:].indirect(entries(PART, PART)), COPY)
            for a in (0, HALF):
                nc.scalar.activation(flat2[:, t, a : a + HALF], planes[t][:].indirect(entries(2 * PART + a, HALF)), COPY)
            nc.vector.tensor_copy(grouped[1][:, :, t], flat1[t][:])
            if t == 1:
                nc.vector.tensor_copy(pairs[:, 0, :, :], flat2[:, 0:2, :].rearrange("p e n -> p n e"))
            if t == 2:
                for a in (0, HALF):
                    nc.vector.tensor_copy(pairs[:, 1, a : a + HALF, 0], flat2[:, 2, a : a + HALF])

        for (a, z), share in zip(chunks, SCALAR_ROUNDS):
            cut = z - share
            nc.vector.tensor_copy(rounded[:, a:cut], planes[3][:, a:cut])
            nc.scalar.activation(rounded[:, cut:z], planes[3][:, cut:z], COPY)
        nc.vector.tensor_copy(grouped[0][:, :, 3], planes[3][:].indirect(entries(0, PART)))
        nc.scalar.activation(grouped[1][:, :, 3], rounded[:].indirect(entries(PART, PART)), COPY)
        nc.scalar.activation(pairs[:, 1, :, 1], rounded[:].indirect(entries(2 * PART, PART)), COPY)

        nc.vector.tensor_copy(w_grouped[:], w_raw[:].rearrange("p j m -> p m j"))
        nc.vector.quantize_mx(
            out=w_codes[:].bitcast(FP8X4), scales=w_scales[:], in_=w_grouped[:].rearrange("p m j -> p (m j)")
        )

        sums = {}

        def product(c, n):
            s, a = divmod(c, PART)
            nc.vector.quantize_mx(
                out=codes[:, c : c + n].bitcast(FP8X4),
                scales=scales[:, c : c + n],
                in_=grouped[s][:].rearrange("p n j -> p (n j)")[:, PACK * a : PACK * (a + n)],
            )
            acc = psum.tile([P, BANK], F32, name=f"acc{c}")
            nc.tensor.matmul_mx(
                out=acc[:, 0:n],
                lhsT=w_codes[:].bitcast(FP8X4),
                lhsT_scale=w_scales[:],
                rhs=codes[:, c : c + n].bitcast(FP8X4),
                rhs_scale=scales[:, c : c + n],
                start=True,
                stop=True,
            )
            for a in range(0, n, NARROW):
                sums[c + a] = acc[:, a:n]

        def relu_on_scalar(c, n):
            nc.scalar.activation(kept[:, c : c + n], sums[c][:, 0:n], RELU, bias=bias[:])

        def square_on_scalar(c, n):
            nc.scalar.activation(result[:, c : c + n], kept[:, c : c + n], SQUARE)

        def relu_on_vector(c, n):
            nc.vector.tensor_scalar(kept[:, c : c + n], sums[c][:, 0:n], bias[:], 0.0, ADD, MAX)

        def square_on_vector(c, n):
            nc.vector.tensor_tensor(result[:, c : c + n], kept[:, c : c + n], kept[:, c : c + n], MULT)

        def store(c):
            nc.sync.dma_start(out[:, c : c + WIDE], result[:, c : c + WIDE])

        wide_pieces = 2 * PART // WIDE
        for c, n in PIECES[:wide_pieces]:
            product(c, n)

        grouped.append(keep.tile([P, PART, PACK], BF16, name="grouped2", tag="grouped0", align_bytes=64))
        pair_words = pairs[:].rearrange("p u n e -> p u (n e)").bitcast(I32)
        for a in (0, HALF):
            nc.vector.tensor_copy(
                grouped[2][:, a : a + HALF, :].bitcast(I32),
                pair_words[:, :, a : a + HALF].rearrange("p u n -> p n u"),
            )
        for c, n in PIECES[wide_pieces:]:
            product(c, n)

        alone = wide_pieces - 1
        relu_on_scalar(0, WIDE)
        for i in range(alone):
            if i + 1 < alone:
                relu_on_scalar((i + 1) * WIDE, WIDE)
            square_on_scalar(i * WIDE, WIDE)
            store(i * WIDE)
        for c in range(alone * WIDE, S, NARROW):
            relu_on_vector(c, NARROW)
        for c in range(alone * WIDE, S - WIDE, WIDE):
            square_on_scalar(c, NARROW)
            square_on_scalar(c + NARROW, NARROW)
            store(c)
        for c, n in PIECES[-2:]:
            square_on_vector(c, n)
        store(S - WIDE)
